import numpy as np
import ml_dtypes


def mxq(x, axis, fmt="e4m3"):
    dtype, down = {"e4m3": (ml_dtypes.float8_e4m3fn, 7), "e5m2": (ml_dtypes.float8_e5m2, 14)}[fmt]
    v = np.moveaxis(np.asarray(x, np.float32).astype(ml_dtypes.bfloat16).astype(np.float64), axis, -1)
    blocks = v.reshape(v.shape[:-1] + (-1, 32))
    amax = np.abs(blocks).max(-1, keepdims=True)
    byte = np.maximum(np.where(amax > 0, np.frexp(amax)[1] - 1 + 127, 0) - down, 1)
    scale = np.exp2(byte - 127.0)
    codes = (blocks / scale).astype(np.float32).astype(dtype).astype(np.float64)
    return np.moveaxis((codes * scale).reshape(v.shape), -1, axis)


WIDE = False


def mx_kscale(k):
    if not WIDE:
        return np.ones(k)
    levels = np.array([10, -10, 5, -5, 0])
    if k % 512:
        return np.exp2(np.random.permutation(np.resize(levels, k // 32))).repeat(32)
    a = np.empty((k // 512, 16))
    for p in range(k // 512):
        a[p, :8] = np.random.permutation(np.resize(levels, 8))
        for g in range(8):
            far = levels[np.abs(levels - a[p, g]) >= 10]
            a[p, g + 8] = far[np.random.randint(len(far))]
    return np.exp2(a.ravel()).repeat(32)


def f64(x):
    return np.asarray(x).astype(np.float64)


def striped(idx):
    return np.tile(idx.reshape(-1, 16).T, (8, 1)).astype(np.uint16)


def unstriped(offs):
    return offs[:16].T.reshape(-1).astype(np.int64)


def pack_weight(w):
    k, n = w.shape
    w = f64(np.asarray(w, np.float32).astype(ml_dtypes.bfloat16)).reshape(k // 32, 32, n)
    amax = np.abs(w).max(1)
    byte = np.clip(np.where(amax > 0, np.frexp(amax)[1] - 1 + 127 - 7, 1), 1, 254)
    scaled = (w * np.exp2(127.0 - byte)[:, None, :]).reshape(k, n).astype(np.float32)
    words = np.ascontiguousarray(scaled.reshape(k // 512, 128, 4, n).transpose(0, 1, 3, 2)).astype(ml_dtypes.float8_e4m3fn).view(np.uint8)
    return words, np.ascontiguousarray(byte.astype(np.uint8).reshape(k // 512, 16, n))


def unpack_weight(words, scales):
    g, p, n, _ = words.shape
    vals = np.ascontiguousarray(words).view(ml_dtypes.float8_e4m3fn).astype(np.float64) * np.repeat(np.exp2(scales.astype(np.float64) - 127.0), 8, axis=1)[..., None]
    return vals.transpose(0, 1, 3, 2).reshape(g * 512, n)


E2M1 = np.array([0.0, 0.5, 1.0, 1.5, 2.0, 3.0, 4.0, 6.0, -0.0, -0.5, -1.0, -1.5, -2.0, -3.0, -4.0, -6.0])


def pack_fp4(w):
    k, n = w.shape
    w = f64(np.asarray(w, np.float32).astype(ml_dtypes.bfloat16)).reshape(k // 32, 32, n)
    amax = np.abs(w).max(1)
    mant, ex = np.frexp(amax / 6.0)
    byte = np.clip(np.where(amax > 0, np.where(mant > 0.5, ex, ex - 1) + 127, 1), 1, 254)
    scaled = (w * np.exp2(127.0 - byte)[:, None, :]).reshape(k, n).astype(np.float32)
    c = np.ascontiguousarray(scaled.reshape(k // 512, 128, 4, n).transpose(0, 1, 3, 2)).astype(ml_dtypes.float4_e2m1fn).view(np.uint8) & 0xF
    words = (c[..., 0::2] | (c[..., 1::2] << 4)).reshape(k // 512, 128, 2 * n)
    return np.ascontiguousarray(words), np.ascontiguousarray(byte.astype(np.uint8).reshape(k // 512, 16, n))


def unpack_fp4(words, scales):
    g, _, n = scales.shape
    words = np.ascontiguousarray(words).reshape(g, 128, n, 2)
    nib = np.empty((g, 128, n, 4), np.uint8)
    nib[..., 0::2] = words & 0xF
    nib[..., 1::2] = words >> 4
    vals = E2M1[nib] * np.repeat(np.exp2(scales.astype(np.float64) - 127.0), 8, axis=1)[..., None]
    return vals.transpose(0, 1, 3, 2).reshape(g * 512, n)


K, T, S, N, H, U = 1024, 2048, 512, 128, 512, 1024


def setup_inputs():
    n = np.random.standard_normal
    s = mx_kscale(K)[:, None]
    u = mx_kscale(H)
    packed_xT = pack_weight(n((K, T)) * s)
    packed_w1 = pack_fp4(n((K, H)) / np.sqrt(K) / s)
    packed_w2 = pack_fp4(n((H, N)) / np.sqrt(H) / u[:, None])
    return {
        "x_words": packed_xT[0],
        "x_scales": packed_xT[1],
        "w1_words": packed_w1[0],
        "w1_scales": packed_w1[1],
        "occ": (np.random.uniform(0.5, 2.0, (H, 1))).astype(np.float32),
        "unit": (np.random.uniform(0.6, 1.4, (H, 1)) * u[:, None]).astype(np.float32),
        "w2_words": packed_w2[0],
        "w2_scales": packed_w2[1],
        "offs": striped(np.random.permutation(T)[:S]),
        "at1": striped(np.random.permutation(np.concatenate([np.arange(S), np.random.randint(0, S, U - S)]))),
        "at2": striped(np.random.permutation(np.concatenate([np.arange(S), np.random.randint(0, S, U - S)]))),
    }


def reference(x_words, x_scales, w1_words, w1_scales, occ, unit, w2_words, w2_scales, offs, at1, at2):
    xq = unpack_weight(x_words, x_scales)[:, unstriped(offs)]
    y = unpack_fp4(w1_words, w1_scales).T @ xq
    c1 = y[:, unstriped(at1)]
    c2 = y[:, unstriped(at2)]
    bo = f64(occ) * (c1 * c2)
    ap = np.abs(bo)
    val = ap.reshape(len(ap), -1, 4).sum(axis=2)
    hid = f64(unit) * (bo / (np.repeat(val, 4, axis=1) + 0.5))
    return unpack_fp4(w2_words, w2_scales).T @ mxq(hid, 0, "e4m3")

@@ -1,0 +1,250 @@
+from contextlib import ExitStack
+
+import concourse.mybir as mybir
+
+K, T, S, N, H, U = 1024, 2048, 512, 128, 512, 1024
+FLOPS = 2 * K * H * S + 2 * H * N * U
+
+F32 = mybir.dt.float32
+BF16 = mybir.dt.bfloat16
+I32 = mybir.dt.int32
+U32 = mybir.dt.uint32
+U16 = mybir.dt.uint16
+U8 = mybir.dt.uint8
+FP8X4 = mybir.dt.float8_e4m3fn_x4
+FP4X4 = mybir.dt.float4_e2m1fn_x4
+ALU = mybir.AluOpType
+ACT = mybir.ActivationFunctionType
+
+P = 128
+PACK = 4
+PASSES = K // (P * PACK)
+QUADS = 4
+GROUP = 4
+CHUNKS = (256, 256, 256, 256)
+ROW0 = 24
+LIVE = 100
+LIST_ROWS = 16
+FUSED = 8
+EVAC_V = (1,)
+FACTOR_S = (2, 3,)
+RING = 8
+
+
+def tile_picked_yhueck_val_p_kernel(
+    tc, x_words, x_scales, w1_words, w1_scales, occ, unit, w2_words, w2_scales, offs, at1, at2, out
+):
+    nc = tc.nc
+    with ExitStack() as ctx:
+        keep = ctx.enter_context(tc.tile_pool(name="keep", bufs=1))
+        work = ctx.enter_context(tc.tile_pool(name="work", bufs=2))
+        psum = ctx.enter_context(tc.psum_pool(name="psum", bufs=1))
+
+        offs_sb = keep.tile([P, S // LIST_ROWS], U16, name="offs_sb")
+        at1_sb = keep.tile([P, U // LIST_ROWS], U16, name="at1_sb")
+        at2_sb = keep.tile([P, U // LIST_ROWS], U16, name="at2_sb")
+
+        x_table = [keep.tile([P, T], U32, name="x_table%d" % o, tag="xw%d" % o, align_bytes=64) for o in range(PASSES)]
+        xs_table = keep.tile([P, T], U8, name="xs_table", align_bytes=64)
+        w1_raw = keep.tile([P, PASSES, 2 * H], U8, name="w1_raw", tag="w1w", align_bytes=64)
+        w1s_raw = keep.tile([P, PASSES, H], U8, name="w1s_raw", tag="w1s", align_bytes=64)
+        x_planes = keep.tile([P, PASSES, S], U8, name="x_planes", align_bytes=64)
+        occ_sb = keep.tile([P, PACK], F32, name="occ_sb")
+
+        for q in range(QUADS):
+            nc.vector.memset(xs_table[32 * q : 32 * q + ROW0, :].bitcast(I32), 0)
+        nc.gpsimd.memset(w1s_raw[:].bitcast(I32), 0)
+        nc.vector.memset(x_planes[96:128, :, :].bitcast(I32), 0)
+
+        nc.sync.dma_start(offs_sb[:], offs)
+        for q in range(QUADS):
+            nc.sync.dma_start(
+                xs_table[32 * q + ROW0 : 32 * q + 32, :].bitcast(I32),
+                x_scales[:, 4 * q : 4 * q + 4, :].bitcast(I32),
+            )
+        nc.scalar.dma_start(w1_raw[:].bitcast(I32), w1_words.rearrange("o p b -> p o b").bitcast(I32))
+        nc.scalar.dma_start(occ_sb[:], occ.rearrange("(p t) one -> p (t one)", t=PACK))
+        nc.sync.dma_start(x_table[0][:].bitcast(I32), x_words[0].rearrange("p c r -> p (c r)").bitcast(I32))
+        nc.sync.dma_start(at1_sb[:], at1)
+        nc.sync.dma_start(at2_sb[:], at2)
+        nc.sync.dma_start(x_table[1][:].bitcast(I32), x_words[1].rearrange("p c r -> p (c r)").bitcast(I32))
+        for q in range(QUADS):
+            nc.scalar.dma_start(
+                w1s_raw[32 * q : 32 * q + 4, :, :].bitcast(I32),
+                w1_scales[:, 4 * q : 4 * q + 4, :].rearrange("o q c -> q o c").bitcast(I32),
+            )
+
+        guess = keep.tile([P, PACK], F32, name="guess")
+        nc.scalar.activation(guess[:], occ_sb[:], ACT.Abs_reciprocal_sqrt)
+        twice = keep.tile([P, PACK], F32, name="twice")
+        nc.gpsimd.tensor_scalar(twice[:], occ_sb[:], 0.0, 2.0, ALU.is_ge, ALU.mult)
+        sign = keep.tile([P, PACK], F32, name="sign")
+        nc.gpsimd.tensor_scalar(sign[:], twice[:], -1.0, 1.0, ALU.add, ALU.mult)
+        size = keep.tile([P, PACK], F32, name="size")
+        nc.gpsimd.tensor_tensor(size[:], occ_sb[:], sign[:], ALU.mult)
+        inv_root = keep.tile([P, PACK], F32, name="inv_root")
+        nc.gpsimd.tensor_scalar(inv_root[:], guess[:], 2.0**63, 0.0, ALU.min, ALU.max)
+        for step in range(1):
+            a = keep.tile([P, PACK], F32, name="nw_a%d" % step)
+            nc.gpsimd.tensor_tensor(a[:], size[:], inv_root[:], ALU.mult)
+            b = keep.tile([P, PACK], F32, name="nw_b%d" % step)
+            nc.gpsimd.tensor_tensor(b[:], a[:], inv_root[:], ALU.mult)
+            c = keep.tile([P, PACK], F32, name="nw_c%d" % step)
+            nc.gpsimd.tensor_scalar(c[:], b[:], -0.5, 1.5, ALU.mult, ALU.add)
+            better = keep.tile([P, PACK], F32, name="nw_d%d" % step)
+            nc.gpsimd.tensor_tensor(better[:], inv_root[:], c[:], ALU.mult)
+            inv_root = better
+        root = keep.tile([P, PACK], F32, name="root")
+        nc.gpsimd.tensor_tensor(root[:], size[:], inv_root[:], ALU.mult)
+
+        xs_picked = keep.tile([P, S], U8, name="xs_picked", align_bytes=64)
+        nc.vector.tensor_copy(xs_picked[:], xs_table[:].indirect(offs_sb[:]))
+        for o in range(PASSES):
+            first = ROW0 + 4 * o
+            nc.scalar.dma_start(x_planes[0:LIVE, o, :].bitcast(I32), xs_picked[first : first + LIVE, :].bitcast(I32))
+        w1_dealt = [keep.tile([P, 2 * H], U8, name="w1_dealt%d" % o, align_bytes=64) for o in range(PASSES)]
+        for o in range(PASSES):
+            nc.vector.tensor_copy(
+                w1_dealt[o][:].rearrange("p (t m b) -> p t m b", t=PACK, b=2),
+                w1_raw[:, o, :].rearrange("p (m t b) -> p t m b", t=PACK, b=2),
+            )
+        x_picked = [keep.tile([P, S], U32, name="x_picked%d" % o, align_bytes=64) for o in range(PASSES)]
+        nc.vector.tensor_copy(x_picked[0][:], x_table[0][:].indirect(offs_sb[:]))
+        w1s_dealt = keep.tile([P, PASSES, H], U8, name="w1s_dealt", align_bytes=64)
+        nc.vector.tensor_copy(
+            w1s_dealt[:].rearrange("p o (t m) -> p o t m", t=PACK),
+            w1s_raw[:].rearrange("p o (m t) -> p o t m", t=PACK),
+        )
+        nc.vector.tensor_copy(x_picked[1][:], x_table[1][:].indirect(offs_sb[:]))
+
+        w2s_sb = keep.tile([P, N], U8, name="w2s_sb", tag="xw0", align_bytes=64)
+        nc.gpsimd.memset(w2s_sb[:].bitcast(I32), 0)
+        for q in range(QUADS):
+            nc.sync.dma_start(w2s_sb[32 * q : 32 * q + 4, :].bitcast(I32), w2_scales[0, 4 * q : 4 * q + 4, :].bitcast(I32))
+        w2_sb = keep.tile([P, 2 * N], U8, name="w2_sb", tag="w1w", align_bytes=64)
+        nc.sync.dma_start(w2_sb[:].bitcast(I32), w2_words[0].bitcast(I32))
+        unit_sb = keep.tile([P, PACK], F32, name="unit_sb", tag="w1s", align_bytes=64)
+        nc.sync.dma_start(unit_sb[:], unit.rearrange("(p t) one -> p (t one)", t=PACK))
+        signed_unit = keep.tile([P, PACK], F32, name="signed_unit")
+        nc.gpsimd.tensor_tensor(signed_unit[:], unit_sb[:], sign[:], ALU.mult)
+
+        banks = [psum.tile([P, S], F32, name="y_bank%d" % t) for t in range(PACK)]
+        for o in range(PASSES):
+            for t in range(PACK):
+                nc.tensor.matmul_mx(
+                    banks[t][:],
+                    lhsT=w1_dealt[o][:, 2 * P * t : 2 * P * (t + 1)].bitcast(FP4X4),
+                    lhsT_scale=w1s_dealt[:, o, P * t : P * (t + 1)],
+                    rhs=x_picked[o][:].bitcast(FP8X4),
+                    rhs_scale=x_planes[:, o, :],
+                    start=(o == 0),
+                    stop=(o == PASSES - 1),
+                )
+        y = [keep.tile([P, S], F32, name="y%d" % t, align_bytes=64) for t in range(PACK)]
+        for t in range(PACK):
+            if t not in EVAC_V:
+                nc.scalar.activation(y[t][:], banks[t][:], ACT.Copy, scale=root[:, t : t + 1])
+            else:
+                nc.vector.tensor_scalar(y[t][:], banks[t][:], root[:, t : t + 1], None, ALU.mult)
+
+        starts = [sum(CHUNKS[:c]) for c in range(len(CHUNKS))]
+        bonds, roots, factors, hids, vals = {}, {}, {}, {}, {}
+
+        def piece(c, t):
+            w = CHUNKS[c]
+            lo, hi = starts[c] // LIST_ROWS, (starts[c] + w) // LIST_ROWS
+            if t == 0:
+                bonds[c] = work.tile([P, PACK, w], F32, name="bond", bufs=3, align_bytes=64)
+            c1 = work.tile([P, w], F32, name="coef", bufs=RING, align_bytes=64)
+            if (c, t) == (0, 1):
+                nc.vector.tensor_copy(c1[:], y[t][:].indirect(at1_sb[:, lo:hi]))
+            else:
+                nc.scalar.activation(c1[:], y[t][:].indirect(at1_sb[:, lo:hi]), ACT.Copy)
+            if PACK * c + t < FUSED:
+                nc.vector.tensor_tensor(bonds[c][:, t, :], y[t][:].indirect(at2_sb[:, lo:hi]), c1[:], ALU.mult)
+            else:
+                c2 = work.tile([P, w], F32, name="coef", bufs=RING, align_bytes=64)
+                nc.scalar.activation(c2[:], y[t][:].indirect(at2_sb[:, lo:hi]), ACT.Copy)
+                nc.vector.tensor_tensor(bonds[c][:, t, :], c1[:], c2[:], ALU.mult)
+            if False:
+                half(c, 0, 2)
+
+        def half(c, t0, t1):
+            groups = CHUNKS[c] // GROUP
+            if t0 == 0:
+                vals[c] = work.tile([P, PACK * groups], F32, name="val", align_bytes=64)
+            nc.vector.tensor_reduce(
+                vals[c][:, t0 * groups : t1 * groups],
+                bonds[c][:, t0:t1, :].rearrange("p t (v d) -> p (t v) d", d=GROUP),
+                mybir.AxisListType.X,
+                ALU.add,
+                apply_absolute_value=True,
+            )
+
+        def valence(c):
+            groups = CHUNKS[c] // GROUP
+            half(c, 0, PACK)
+            g = work.tile([P, PACK, groups], F32, name="g", align_bytes=64)
+            nc.scalar.activation(g[:].rearrange("p t v -> p (t v)"), vals[c][:], ACT.Abs_reciprocal_sqrt, bias=0.5)
+            roots[c] = g
+            if c in FACTOR_S:
+                sq = work.tile([P, PACK, groups], F32, name="sq", align_bytes=64)
+                nc.scalar.activation(sq[:], g[:], ACT.Square)
+                factors[c] = work.tile([P, PACK, groups], F32, name="factor", align_bytes=64)
+                for t in range(PACK):
+                    nc.scalar.activation(factors[c][:, t, :], sq[:, t, :], ACT.Copy, scale=signed_unit[:, t : t + 1])
+
+        def factor(c):
+            if c in FACTOR_S:
+                return
+            g = roots[c]
+            factors[c] = work.tile([P, PACK, CHUNKS[c] // GROUP], F32, name="factor", align_bytes=64)
+            for t in range(PACK):
+                nc.vector.scalar_tensor_tensor(
+                    factors[c][:, t, :], g[:, t, :], signed_unit[:, t : t + 1], g[:, t, :], ALU.mult, ALU.mult
+                )
+
+        def normalise(c):
+            w = CHUNKS[c]
+            hids[c] = work.tile([P, w * PACK], BF16, name="hid", align_bytes=64)
+            nc.vector.tensor_tensor(
+                hids[c][:].rearrange("p (v d t) -> p v t d", d=GROUP, t=PACK),
+                bonds[c][:].rearrange("p t (v d) -> p v t d", d=GROUP),
+                factors[c][:].rearrange("p t v -> p v t").unsqueeze(3).to_broadcast([P, w // GROUP, PACK, GROUP]),
+                ALU.mult,
+            )
+
+        def transform(c):
+            w = CHUNKS[c]
+            codes = work.tile([P, w], U32, name="codes", align_bytes=64)
+            scales = work.tile([P, w], U8, name="scales", align_bytes=64)
+            nc.vector.quantize_mx(codes[:].bitcast(FP8X4), scales[:], hids[c][:])
+            acc = psum.tile([P, w], F32, name="acc", bufs=2)
+            nc.tensor.matmul_mx(
+                acc[:],
+                lhsT=w2_sb[:].bitcast(FP4X4),
+                lhsT_scale=w2s_sb[:],
+                rhs=codes[:].bitcast(FP8X4),
+                rhs_scale=scales[:],
+                start=True,
+                stop=True,
+            )
+            res = work.tile([P, w], F32, name="res", align_bytes=64)
+            nc.scalar.copy(res[:], acc[:])
+            nc.sync.dma_start(out[:, starts[c] : starts[c] + w], res[:])
+
+        n = len(CHUNKS)
+        for c in range(n + 1):
+            for s in range(6):
+                if c > 0:
+                    if s == 3:
+                        factor(c - 1)
+                    if s == 4:
+                        normalise(c - 1)
+                    if s == 5:
+                        transform(c - 1)
+                if c < n:
+                    if s < PACK:
+                        piece(c, s)
+                    if s == PACK:
+                        valence(c)

@@ -52,9 +52,10 @@ def tile_picked_yhueck_val_p_kernel(
         occ_sb = keep.tile([P, PACK], F32, name="occ_sb")
 
         for q in range(QUADS):
-            nc.vector.memset(xs_table[32 * q : 32 * q + ROW0, :].bitcast(I32), 0)
-        nc.gpsimd.memset(w1s_raw[:].bitcast(I32), 0)
-        nc.vector.memset(x_planes[96:128, :, :].bitcast(I32), 0)
+            engine = nc.gpsimd if q < 2 else nc.vector
+            engine.memset(xs_table[32 * q : 32 * q + ROW0, :].bitcast(I32), 0)
+        nc.vector.memset(w1s_raw[:].bitcast(I32), 0)
+        nc.gpsimd.memset(x_planes[96:128, :, :].bitcast(I32), 0)
 
         nc.sync.dma_start(offs_sb[:], offs)
         for q in range(QUADS):
@@ -103,19 +104,18 @@ def tile_picked_yhueck_val_p_kernel(
             first = ROW0 + 4 * o
             nc.scalar.dma_start(x_planes[0:LIVE, o, :].bitcast(I32), xs_picked[first : first + LIVE, :].bitcast(I32))
         w1_dealt = [keep.tile([P, 2 * H], U8, name="w1_dealt%d" % o, align_bytes=64) for o in range(PASSES)]
+        w1s_dealt = [keep.tile([P, H], U8, name="w1s_dealt%d" % o, align_bytes=64) for o in range(PASSES)]
+        x_picked = [keep.tile([P, S], U32, name="x_picked%d" % o, align_bytes=64) for o in range(PASSES)]
         for o in range(PASSES):
             nc.vector.tensor_copy(
-                w1_dealt[o][:].rearrange("p (t m b) -> p t m b", t=PACK, b=2),
-                w1_raw[:, o, :].rearrange("p (m t b) -> p t m b", t=PACK, b=2),
+                w1_dealt[o][:].bitcast(U16).rearrange("p (t m) -> p t m", t=PACK),
+                w1_raw[:, o, :].bitcast(U16).rearrange("p (m t) -> p t m", t=PACK),
             )
-        x_picked = [keep.tile([P, S], U32, name="x_picked%d" % o, align_bytes=64) for o in range(PASSES)]
-        nc.vector.tensor_copy(x_picked[0][:], x_table[0][:].indirect(offs_sb[:]))
-        w1s_dealt = keep.tile([P, PASSES, H], U8, name="w1s_dealt", align_bytes=64)
-        nc.vector.tensor_copy(
-            w1s_dealt[:].rearrange("p o (t m) -> p o t m", t=PACK),
-            w1s_raw[:].rearrange("p o (m t) -> p o t m", t=PACK),
-        )
-        nc.vector.tensor_copy(x_picked[1][:], x_table[1][:].indirect(offs_sb[:]))
+            nc.vector.tensor_copy(
+                w1s_dealt[o][:].rearrange("p (t m) -> p t m", t=PACK),
+                w1s_raw[:, o, :].rearrange("p (m t) -> p t m", t=PACK),
+            )
+            nc.vector.tensor_copy(x_picked[o][:], x_table[o][:].indirect(offs_sb[:]))
 
         w2s_sb = keep.tile([P, N], U8, name="w2s_sb", tag="xw0", align_bytes=64)
         nc.gpsimd.memset(w2s_sb[:].bitcast(I32), 0)
@@ -128,24 +128,23 @@ def tile_picked_yhueck_val_p_kernel(
         signed_unit = keep.tile([P, PACK], F32, name="signed_unit")
         nc.gpsimd.tensor_tensor(signed_unit[:], unit_sb[:], sign[:], ALU.mult)
 
-        banks = [psum.tile([P, S], F32, name="y_bank%d" % t) for t in range(PACK)]
-        for o in range(PASSES):
-            for t in range(PACK):
+        y = [keep.tile([P, S], F32, name="y%d" % t, align_bytes=64) for t in range(PACK)]
+        for t in range(PACK):
+            bank = psum.tile([P, S], F32, name="y_bank", bufs=4)
+            for o in range(PASSES):
                 nc.tensor.matmul_mx(
-                    banks[t][:],
+                    bank[:],
                     lhsT=w1_dealt[o][:, 2 * P * t : 2 * P * (t + 1)].bitcast(FP4X4),
-                    lhsT_scale=w1s_dealt[:, o, P * t : P * (t + 1)],
+                    lhsT_scale=w1s_dealt[o][:, P * t : P * (t + 1)],
                     rhs=x_picked[o][:].bitcast(FP8X4),
                     rhs_scale=x_planes[:, o, :],
                     start=(o == 0),
                     stop=(o == PASSES - 1),
                 )
-        y = [keep.tile([P, S], F32, name="y%d" % t, align_bytes=64) for t in range(PACK)]
-        for t in range(PACK):
             if t not in EVAC_V:
-                nc.scalar.activation(y[t][:], banks[t][:], ACT.Copy, scale=root[:, t : t + 1])
+                nc.scalar.activation(y[t][:], bank[:], ACT.Copy, scale=root[:, t : t + 1])
             else:
-                nc.vector.tensor_scalar(y[t][:], banks[t][:], root[:, t : t + 1], None, ALU.mult)
+                nc.vector.tensor_scalar(y[t][:], bank[:], root[:, t : t + 1], None, ALU.mult)
 
         starts = [sum(CHUNKS[:c]) for c in range(len(CHUNKS))]
         bonds, roots, factors, hids, vals = {}, {}, {}, {}, {}
@@ -208,9 +207,9 @@ def tile_picked_yhueck_val_p_kernel(
             w = CHUNKS[c]
             hids[c] = work.tile([P, w * PACK], BF16, name="hid", align_bytes=64)
             nc.vector.tensor_tensor(
-                hids[c][:].rearrange("p (v d t) -> p v t d", d=GROUP, t=PACK),
-                bonds[c][:].rearrange("p t (v d) -> p v t d", d=GROUP),
-                factors[c][:].rearrange("p t v -> p v t").unsqueeze(3).to_broadcast([P, w // GROUP, PACK, GROUP]),
+                hids[c][:].rearrange("p (v d t) -> p v d t", d=GROUP, t=PACK),
+                bonds[c][:].rearrange("p t (v d) -> p v d t", d=GROUP),
+                factors[c][:].rearrange("p t v -> p v t").unsqueeze(2).to_broadcast([P, w // GROUP, GROUP, PACK]),
                 ALU.mult,
             )
 

@@ -203,34 +203,44 @@ def tile_picked_yhueck_val_p_kernel(
                     factors[c][:, t, :], g[:, t, :], signed_unit[:, t : t + 1], g[:, t, :], ALU.mult, ALU.mult
                 )
 
-        def normalise(c):
+        def spans(c):
             w = CHUNKS[c]
-            hids[c] = work.tile([P, w * PACK], BF16, name="hid", align_bytes=64)
-            nc.vector.tensor_tensor(
-                hids[c][:].rearrange("p (v d t) -> p v d t", d=GROUP, t=PACK),
-                bonds[c][:].rearrange("p t (v d) -> p v d t", d=GROUP),
-                factors[c][:].rearrange("p t v -> p v t").unsqueeze(2).to_broadcast([P, w // GROUP, GROUP, PACK]),
-                ALU.mult,
-            )
+            parts = 2 if c == len(CHUNKS) - 1 else 1
+            return [(k * w // parts, (k + 1) * w // parts) for k in range(parts)]
+
+        def normalise(c):
+            for lo, hi in spans(c):
+                w = hi - lo
+                hids[c, lo] = work.tile([P, w * PACK], BF16, name="hid", bufs=3, align_bytes=64)
+                nc.vector.tensor_tensor(
+                    hids[c, lo][:].rearrange("p (v d t) -> p v t d", d=GROUP, t=PACK),
+                    bonds[c][:, :, lo:hi].rearrange("p t (v d) -> p v t d", d=GROUP),
+                    factors[c][:, :, lo // GROUP : hi // GROUP]
+                    .rearrange("p t v -> p v t")
+                    .unsqueeze(3)
+                    .to_broadcast([P, w // GROUP, PACK, GROUP]),
+                    ALU.mult,
+                )
 
         def transform(c):
-            w = CHUNKS[c]
-            codes = work.tile([P, w], U32, name="codes", align_bytes=64)
-            scales = work.tile([P, w], U8, name="scales", align_bytes=64)
-            nc.vector.quantize_mx(codes[:].bitcast(FP8X4), scales[:], hids[c][:])
-            acc = psum.tile([P, w], F32, name="acc", bufs=2)
-            nc.tensor.matmul_mx(
-                acc[:],
-                lhsT=w2_sb[:].bitcast(FP4X4),
-                lhsT_scale=w2s_sb[:],
-                rhs=codes[:].bitcast(FP8X4),
-                rhs_scale=scales[:],
-                start=True,
-                stop=True,
-            )
-            res = work.tile([P, w], F32, name="res", align_bytes=64)
-            nc.scalar.copy(res[:], acc[:])
-            nc.sync.dma_start(out[:, starts[c] : starts[c] + w], res[:])
+            for lo, hi in spans(c):
+                w = hi - lo
+                codes = work.tile([P, w], U32, name="codes", align_bytes=64)
+                scales = work.tile([P, w], U8, name="scales", align_bytes=64)
+                nc.vector.quantize_mx(codes[:].bitcast(FP8X4), scales[:], hids[c, lo][:])
+                acc = psum.tile([P, w], F32, name="acc", bufs=2)
+                nc.tensor.matmul_mx(
+                    acc[:],
+                    lhsT=w2_sb[:].bitcast(FP4X4),
+                    lhsT_scale=w2s_sb[:],
+                    rhs=codes[:].bitcast(FP8X4),
+                    rhs_scale=scales[:],
+                    start=True,
+                    stop=True,
+                )
+                res = work.tile([P, w], F32, name="res", bufs=3, align_bytes=64)
+                nc.scalar.copy(res[:], acc[:])
+                nc.sync.dma_start(out[:, starts[c] + lo : starts[c] + hi], res[:])
 
         n = len(CHUNKS)
         for c in range(n + 1):

from contextlib import ExitStack

import concourse.mybir as mybir

K, T, S, N, H, U = 1024, 2048, 512, 128, 512, 1024
FLOPS = 2 * K * H * S + 2 * H * N * U

F32 = mybir.dt.float32
BF16 = mybir.dt.bfloat16
I32 = mybir.dt.int32
U32 = mybir.dt.uint32
U16 = mybir.dt.uint16
U8 = mybir.dt.uint8
FP8X4 = mybir.dt.float8_e4m3fn_x4
FP4X4 = mybir.dt.float4_e2m1fn_x4
ALU = mybir.AluOpType
ACT = mybir.ActivationFunctionType

P = 128
PACK = 4
PASSES = K // (P * PACK)
QUADS = 4
GROUP = 4
CHUNKS = (256, 256, 256, 256)
ROW0 = 24
LIVE = 100
LIST_ROWS = 16
FUSED = 8
EVAC_V = (1,)
FACTOR_S = (2, 3,)
RING = 8


def tile_picked_yhueck_val_p_kernel(
    tc, x_words, x_scales, w1_words, w1_scales, occ, unit, w2_words, w2_scales, offs, at1, at2, out
):
    nc = tc.nc
    with ExitStack() as ctx:
        keep = ctx.enter_context(tc.tile_pool(name="keep", bufs=1))
        work = ctx.enter_context(tc.tile_pool(name="work", bufs=2))
        psum = ctx.enter_context(tc.psum_pool(name="psum", bufs=1))

        offs_sb = keep.tile([P, S // LIST_ROWS], U16, name="offs_sb")
        at1_sb = keep.tile([P, U // LIST_ROWS], U16, name="at1_sb")
        at2_sb = keep.tile([P, U // LIST_ROWS], U16, name="at2_sb")

        x_table = [keep.tile([P, T], U32, name="x_table%d" % o, tag="xw%d" % o, align_bytes=64) for o in range(PASSES)]
        xs_table = keep.tile([P, T], U8, name="xs_table", align_bytes=64)
        w1_raw = keep.tile([P, PASSES, 2 * H], U8, name="w1_raw", tag="w1w", align_bytes=64)
        w1s_raw = keep.tile([P, PASSES, H], U8, name="w1s_raw", tag="w1s", align_bytes=64)
        x_planes = keep.tile([P, PASSES, S], U8, name="x_planes", align_bytes=64)
        occ_sb = keep.tile([P, PACK], F32, name="occ_sb")

        for q in range(QUADS):
            engine = nc.gpsimd if q < 2 else nc.vector
            engine.memset(xs_table[32 * q : 32 * q + ROW0, :].bitcast(I32), 0)
        nc.vector.memset(w1s_raw[:].bitcast(I32), 0)
        nc.gpsimd.memset(x_planes[96:128, :, :].bitcast(I32), 0)

        nc.sync.dma_start(offs_sb[:], offs)
        for q in range(QUADS):
            nc.sync.dma_start(
                xs_table[32 * q + ROW0 : 32 * q + 32, :].bitcast(I32),
                x_scales[:, 4 * q : 4 * q + 4, :].bitcast(I32),
            )
        nc.scalar.dma_start(w1_raw[:].bitcast(I32), w1_words.rearrange("o p b -> p o b").bitcast(I32))
        nc.scalar.dma_start(occ_sb[:], occ.rearrange("(p t) one -> p (t one)", t=PACK))
        nc.sync.dma_start(x_table[0][:].bitcast(I32), x_words[0].rearrange("p c r -> p (c r)").bitcast(I32))
        nc.sync.dma_start(at1_sb[:], at1)
        nc.sync.dma_start(at2_sb[:], at2)
        nc.sync.dma_start(x_table[1][:].bitcast(I32), x_words[1].rearrange("p c r -> p (c r)").bitcast(I32))
        for q in range(QUADS):
            nc.scalar.dma_start(
                w1s_raw[32 * q : 32 * q + 4, :, :].bitcast(I32),
                w1_scales[:, 4 * q : 4 * q + 4, :].rearrange("o q c -> q o c").bitcast(I32),
            )

        guess = keep.tile([P, PACK], F32, name="guess")
        nc.scalar.activation(guess[:], occ_sb[:], ACT.Abs_reciprocal_sqrt)
        twice = keep.tile([P, PACK], F32, name="twice")
        nc.gpsimd.tensor_scalar(twice[:], occ_sb[:], 0.0, 2.0, ALU.is_ge, ALU.mult)
        sign = keep.tile([P, PACK], F32, name="sign")
        nc.gpsimd.tensor_scalar(sign[:], twice[:], -1.0, 1.0, ALU.add, ALU.mult)
        size = keep.tile([P, PACK], F32, name="size")
        nc.gpsimd.tensor_tensor(size[:], occ_sb[:], sign[:], ALU.mult)
        inv_root = keep.tile([P, PACK], F32, name="inv_root")
        nc.gpsimd.tensor_scalar(inv_root[:], guess[:], 2.0**63, 0.0, ALU.min, ALU.max)
        for step in range(1):
            a = keep.tile([P, PACK], F32, name="nw_a%d" % step)
            nc.gpsimd.tensor_tensor(a[:], size[:], inv_root[:], ALU.mult)
            b = keep.tile([P, PACK], F32, name="nw_b%d" % step)
            nc.gpsimd.tensor_tensor(b[:], a[:], inv_root[:], ALU.mult)
            c = keep.tile([P, PACK], F32, name="nw_c%d" % step)
            nc.gpsimd.tensor_scalar(c[:], b[:], -0.5, 1.5, ALU.mult, ALU.add)
            better = keep.tile([P, PACK], F32, name="nw_d%d" % step)
            nc.gpsimd.tensor_tensor(better[:], inv_root[:], c[:], ALU.mult)
            inv_root = better
        root = keep.tile([P, PACK], F32, name="root")
        nc.gpsimd.tensor_tensor(root[:], size[:], inv_root[:], ALU.mult)

        xs_picked = keep.tile([P, S], U8, name="xs_picked", align_bytes=64)
        nc.vector.tensor_copy(xs_picked[:], xs_table[:].indirect(offs_sb[:]))
        for o in range(PASSES):
            first = ROW0 + 4 * o
            nc.scalar.dma_start(x_planes[0:LIVE, o, :].bitcast(I32), xs_picked[first : first + LIVE, :].bitcast(I32))
        w1_dealt = [keep.tile([P, 2 * H], U8, name="w1_dealt%d" % o, align_bytes=64) for o in range(PASSES)]
        w1s_dealt = [keep.tile([P, H], U8, name="w1s_dealt%d" % o, align_bytes=64) for o in range(PASSES)]
        x_picked = [keep.tile([P, S], U32, name="x_picked%d" % o, align_bytes=64) for o in range(PASSES)]
        for o in range(PASSES):
            nc.vector.tensor_copy(
                w1_dealt[o][:].bitcast(U16).rearrange("p (t m) -> p t m", t=PACK),
                w1_raw[:, o, :].bitcast(U16).rearrange("p (m t) -> p t m", t=PACK),
            )
            nc.vector.tensor_copy(
                w1s_dealt[o][:].rearrange("p (t m) -> p t m", t=PACK),
                w1s_raw[:, o, :].rearrange("p (m t) -> p t m", t=PACK),
            )
            nc.vector.tensor_copy(x_picked[o][:], x_table[o][:].indirect(offs_sb[:]))

        w2s_sb = keep.tile([P, N], U8, name="w2s_sb", tag="xw0", align_bytes=64)
        nc.gpsimd.memset(w2s_sb[:].bitcast(I32), 0)
        for q in range(QUADS):
            nc.sync.dma_start(w2s_sb[32 * q : 32 * q + 4, :].bitcast(I32), w2_scales[0, 4 * q : 4 * q + 4, :].bitcast(I32))
        w2_sb = keep.tile([P, 2 * N], U8, name="w2_sb", tag="w1w", align_bytes=64)
        nc.sync.dma_start(w2_sb[:].bitcast(I32), w2_words[0].bitcast(I32))
        unit_sb = keep.tile([P, PACK], F32, name="unit_sb", tag="w1s", align_bytes=64)
        nc.sync.dma_start(unit_sb[:], unit.rearrange("(p t) one -> p (t one)", t=PACK))
        signed_unit = keep.tile([P, PACK], F32, name="signed_unit")
        nc.gpsimd.tensor_tensor(signed_unit[:], unit_sb[:], sign[:], ALU.mult)

        y = [keep.tile([P, S], F32, name="y%d" % t, align_bytes=64) for t in range(PACK)]
        for t in range(PACK):
            bank = psum.tile([P, S], F32, name="y_bank", bufs=4)
            for o in range(PASSES):
                nc.tensor.matmul_mx(
                    bank[:],
                    lhsT=w1_dealt[o][:, 2 * P * t : 2 * P * (t + 1)].bitcast(FP4X4),
                    lhsT_scale=w1s_dealt[o][:, P * t : P * (t + 1)],
                    rhs=x_picked[o][:].bitcast(FP8X4),
                    rhs_scale=x_planes[:, o, :],
                    start=(o == 0),
                    stop=(o == PASSES - 1),
                )
            if t not in EVAC_V:
                nc.scalar.activation(y[t][:], bank[:], ACT.Copy, scale=root[:, t : t + 1])
            else:
                nc.vector.tensor_scalar(y[t][:], bank[:], root[:, t : t + 1], None, ALU.mult)

        starts = [sum(CHUNKS[:c]) for c in range(len(CHUNKS))]
        bonds, roots, factors, hids, vals = {}, {}, {}, {}, {}

        def piece(c, t):
            w = CHUNKS[c]
            lo, hi = starts[c] // LIST_ROWS, (starts[c] + w) // LIST_ROWS
            if t == 0:
                bonds[c] = work.tile([P, PACK, w], F32, name="bond", bufs=3, align_bytes=64)
            c1 = work.tile([P, w], F32, name="coef", bufs=RING, align_bytes=64)
            if (c, t) == (0, 1):
                nc.vector.tensor_copy(c1[:], y[t][:].indirect(at1_sb[:, lo:hi]))
            else:
                nc.scalar.activation(c1[:], y[t][:].indirect(at1_sb[:, lo:hi]), ACT.Copy)
            if PACK * c + t < FUSED:
                nc.vector.tensor_tensor(bonds[c][:, t, :], y[t][:].indirect(at2_sb[:, lo:hi]), c1[:], ALU.mult)
            else:
                c2 = work.tile([P, w], F32, name="coef", bufs=RING, align_bytes=64)
                nc.scalar.activation(c2[:], y[t][:].indirect(at2_sb[:, lo:hi]), ACT.Copy)
                nc.vector.tensor_tensor(bonds[c][:, t, :], c1[:], c2[:], ALU.mult)
            if False:
                half(c, 0, 2)

        def half(c, t0, t1):
            groups = CHUNKS[c] // GROUP
            if t0 == 0:
                vals[c] = work.tile([P, PACK * groups], F32, name="val", align_bytes=64)
            nc.vector.tensor_reduce(
                vals[c][:, t0 * groups : t1 * groups],
                bonds[c][:, t0:t1, :].rearrange("p t (v d) -> p (t v) d", d=GROUP),
                mybir.AxisListType.X,
                ALU.add,
                apply_absolute_value=True,
            )

        def valence(c):
            groups = CHUNKS[c] // GROUP
            half(c, 0, PACK)
            g = work.tile([P, PACK, groups], F32, name="g", align_bytes=64)
            nc.scalar.activation(g[:].rearrange("p t v -> p (t v)"), vals[c][:], ACT.Abs_reciprocal_sqrt, bias=0.5)
            roots[c] = g
            if c in FACTOR_S:
                sq = work.tile([P, PACK, groups], F32, name="sq", align_bytes=64)
                nc.scalar.activation(sq[:], g[:], ACT.Square)
                factors[c] = work.tile([P, PACK, groups], F32, name="factor", align_bytes=64)
                for t in range(PACK):
                    nc.scalar.activation(factors[c][:, t, :], sq[:, t, :], ACT.Copy, scale=signed_unit[:, t : t + 1])

        def factor(c):
            if c in FACTOR_S:
                return
            g = roots[c]
            factors[c] = work.tile([P, PACK, CHUNKS[c] // GROUP], F32, name="factor", align_bytes=64)
            for t in range(PACK):
                nc.vector.scalar_tensor_tensor(
                    factors[c][:, t, :], g[:, t, :], signed_unit[:, t : t + 1], g[:, t, :], ALU.mult, ALU.mult
                )

        def spans(c):
            w = CHUNKS[c]
            parts = 2 if c == len(CHUNKS) - 1 else 1
            return [(k * w // parts, (k + 1) * w // parts) for k in range(parts)]

        def normalise(c):
            for lo, hi in spans(c):
                w = hi - lo
                hids[c, lo] = work.tile([P, w * PACK], BF16, name="hid", bufs=3, align_bytes=64)
                nc.vector.tensor_tensor(
                    hids[c, lo][:].rearrange("p (v d t) -> p v t d", d=GROUP, t=PACK),
                    bonds[c][:, :, lo:hi].rearrange("p t (v d) -> p v t d", d=GROUP),
                    factors[c][:, :, lo // GROUP : hi // GROUP]
                    .rearrange("p t v -> p v t")
                    .unsqueeze(3)
                    .to_broadcast([P, w // GROUP, PACK, GROUP]),
                    ALU.mult,
                )

        def transform(c):
            for lo, hi in spans(c):
                w = hi - lo
                codes = work.tile([P, w], U32, name="codes", align_bytes=64)
                scales = work.tile([P, w], U8, name="scales", align_bytes=64)
                nc.vector.quantize_mx(codes[:].bitcast(FP8X4), scales[:], hids[c, lo][:])
                acc = psum.tile([P, w], F32, name="acc", bufs=2)
                nc.tensor.matmul_mx(
                    acc[:],
                    lhsT=w2_sb[:].bitcast(FP4X4),
                    lhsT_scale=w2s_sb[:],
                    rhs=codes[:].bitcast(FP8X4),
                    rhs_scale=scales[:],
                    start=True,
                    stop=True,
                )
                res = work.tile([P, w], F32, name="res", bufs=3, align_bytes=64)
                nc.scalar.copy(res[:], acc[:])
                nc.sync.dma_start(out[:, starts[c] + lo : starts[c] + hi], res[:])

        n = len(CHUNKS)
        for c in range(n + 1):
            for s in range(6):
                if c > 0:
                    if s == 3:
                        factor(c - 1)
                    if s == 4:
                        normalise(c - 1)
                    if s == 5:
                        transform(c - 1)
                if c < n:
                    if s < PACK:
                        piece(c, s)
                    if s == PACK:
                        valence(c)
